import numpy as np
import ml_dtypes


def mxq(x, axis, fmt="e4m3"):
    dtype, down = {"e4m3": (ml_dtypes.float8_e4m3fn, 7), "e5m2": (ml_dtypes.float8_e5m2, 14)}[fmt]
    v = np.moveaxis(np.asarray(x, np.float32).astype(ml_dtypes.bfloat16).astype(np.float64), axis, -1)
    blocks = v.reshape(v.shape[:-1] + (-1, 32))
    amax = np.abs(blocks).max(-1, keepdims=True)
    byte = np.maximum(np.where(amax > 0, np.frexp(amax)[1] - 1 + 127, 0) - down, 1)
    scale = np.exp2(byte - 127.0)
    codes = (blocks / scale).astype(np.float32).astype(dtype).astype(np.float64)
    return np.moveaxis((codes * scale).reshape(v.shape), -1, axis)


WIDE = False


def mx_kscale(k):
    if not WIDE:
        return np.ones(k)
    levels = np.array([10, -10, 5, -5, 0])
    if k % 512:
        return np.exp2(np.random.permutation(np.resize(levels, k // 32))).repeat(32)
    a = np.empty((k // 512, 16))
    for p in range(k // 512):
        a[p, :8] = np.random.permutation(np.resize(levels, 8))
        for g in range(8):
            far = levels[np.abs(levels - a[p, g]) >= 10]
            a[p, g + 8] = far[np.random.randint(len(far))]
    return np.exp2(a.ravel()).repeat(32)


def f64(x):
    return np.asarray(x).astype(np.float64)


def striped(idx):
    return np.tile(idx.reshape(-1, 16).T, (8, 1)).astype(np.uint16)


def unstriped(offs):
    return offs[:16].T.reshape(-1).astype(np.int64)


def pack_weight(w):
    k, n = w.shape
    w = f64(np.asarray(w, np.float32).astype(ml_dtypes.bfloat16)).reshape(k // 32, 32, n)
    amax = np.abs(w).max(1)
    byte = np.clip(np.where(amax > 0, np.frexp(amax)[1] - 1 + 127 - 7, 1), 1, 254)
    scaled = (w * np.exp2(127.0 - byte)[:, None, :]).reshape(k, n).astype(np.float32)
    words = np.ascontiguousarray(scaled.reshape(k // 512, 128, 4, n).transpose(0, 1, 3, 2)).astype(ml_dtypes.float8_e4m3fn).view(np.uint8)
    return words, np.ascontiguousarray(byte.astype(np.uint8).reshape(k // 512, 16, n))


def unpack_weight(words, scales):
    g, p, n, _ = words.shape
    vals = np.ascontiguousarray(words).view(ml_dtypes.float8_e4m3fn).astype(np.float64) * np.repeat(np.exp2(scales.astype(np.float64) - 127.0), 8, axis=1)[..., None]
    return vals.transpose(0, 1, 3, 2).reshape(g * 512, n)


def planes(y):
    n, m = y.shape
    v = y.astype(np.float32).astype(ml_dtypes.bfloat16).astype(np.float64).reshape(n // 32, 32, m)
    top = np.abs(v).max(1)
    byte = np.clip(np.where(top > 0, np.frexp(top)[1] - 1 + 127 - 7, 1), 1, 254)
    codes = (v * np.exp2(127.0 - byte)[:, None, :]).reshape(n, m).astype(np.float32).astype(ml_dtypes.float8_e4m3fn).view(np.uint8)
    words = codes.reshape(n // 512, 128, 4, m).transpose(0, 1, 3, 2)
    return np.ascontiguousarray(words), np.ascontiguousarray(byte.astype(np.uint8).reshape(n // 512, 16, m))


def sigmoid(v):
    return 1.0 / (1.0 + np.exp(-np.maximum(v, -700.0)))


K, T, S, N, U = 512, 1024, 512, 512, 1024


def setup_inputs():
    n = np.random.standard_normal
    s = mx_kscale(K)[:, None]
    packed_xT = pack_weight(n((K, T)) * s)
    return {
        "x_words": packed_xT[0],
        "x_scales": packed_xT[1],
        "cell": (n((N, U))).astype(np.float32),
        "w1": (n((K, N)) / np.sqrt(K) / s).astype(np.float32),
        "w2": (n((K, N)) / np.sqrt(K) / s).astype(np.float32),
        "w3": (n((K, N)) / np.sqrt(K) / s).astype(np.float32),
        "peep": (0.5 * n((N, 1))).astype(np.float32),
        "offs": striped(np.random.permutation(T)[:S]),
        "slot": striped(np.random.permutation(U)[:S]),
    }


def reference(x_words, x_scales, cell, w1, w2, w3, peep, offs, slot):
    xq = unpack_weight(x_words, x_scales)[:, unstriped(offs)]
    y = mxq(f64(w2), 0, "e4m3").T @ xq
    rr = sigmoid(mxq(f64(w3), 0, "e4m3").T @ xq)
    old = f64(cell)[:, unstriped(slot)]
    f = sigmoid((mxq(f64(w1), 0, "e4m3").T @ xq) + f64(peep) * old)
    new = y + f * (old - y)
    out_0 = y + rr * (new - y)
    return (out_0,) + planes(out_0)

@@ -1,0 +1,185 @@
+from contextlib import ExitStack
+
+import concourse.mybir as mybir
+
+K, T, S, N, U = 512, 1024, 512, 512, 1024
+FLOPS = 3 * 2 * K * N * S
+
+F32 = mybir.dt.float32
+BF16 = mybir.dt.bfloat16
+I32 = mybir.dt.int32
+U32 = mybir.dt.uint32
+U16 = mybir.dt.uint16
+U8 = mybir.dt.uint8
+FP8X4 = mybir.dt.float8_e4m3fn_x4
+MULT = mybir.AluOpType.mult
+ADD = mybir.AluOpType.add
+SUB = mybir.AluOpType.subtract
+SIGMOID = mybir.ActivationFunctionType.Sigmoid
+
+P = 128
+PACK = 4
+
+
+def tile_picked_ysru_hwy_po_kernel(tc, x_words, x_scales, cell, w1, w2, w3, peep, offs, slot, out_0, out_1, out_2):
+    nc = tc.nc
+    with ExitStack() as ctx:
+        keep = ctx.enter_context(tc.tile_pool(name="keep", bufs=1))
+        psum = ctx.enter_context(tc.psum_pool(name="psum", bufs=1))
+
+        offs_sb = keep.tile([P, S // 16], U16, name="offs_sb")
+        slot_sb = keep.tile([P, S // 16], U16, name="slot_sb")
+        peep_sb = keep.tile([P, PACK], F32, name="peep_sb")
+        xw_all = keep.tile([P, T], U32, name="xw_all")
+        xs_all = keep.tile([P, T], U8, name="xs_all")
+        xw = keep.tile([P, S], U32, name="xw", align_bytes=64)
+        xs = keep.tile([P, S], U8, name="xs", align_bytes=64)
+        cell_sb = [keep.tile([P, U], F32, name="cell%d" % t, tag="cell%d" % t, align_bytes=64) for t in range(PACK)]
+        w_raw = [keep.tile([P, PACK, N], F32, name="w_raw%d" % i) for i in range(3)]
+        w_bf = [keep.tile([P, PACK, P, PACK], BF16, name="w_bf%d" % i, align_bytes=64) for i in range(3)]
+        w_codes = {i: keep.tile([P, N], U32, name="w_codes%d" % i, align_bytes=64) for i in (0, 2)}
+        w_scales = [keep.tile([P, N], U8, name="w_scales%d" % i, align_bytes=64) for i in range(3)]
+        old = keep.tile([P, PACK, S], F32, name="old")
+        fg = w_raw[1]
+        rg = [keep.tile([P, PACK, P], F32, name="rg%d" % c) for c in range(4)]
+        diff = [keep.tile([P, PACK, P], F32, name="diff%d" % c) for c in range(4)]
+        gated = [keep.tile([P, PACK, P], F32, name="gated%d" % c) for c in range(4)]
+        res = [keep.tile([P, PACK, P], F32, name="res%d" % c) for c in range(4)]
+        res_bf = [keep.tile([P, P, PACK], BF16, name="res_bf%d" % c, align_bytes=64) for c in range(4)]
+        res_codes = keep.tile([P, S], U32, name="res_codes", align_bytes=64)
+        res_scales = keep.tile([P, S], U8, name="res_scales", align_bytes=64)
+        warm = keep.tile([P, 1], F32, name="warm")
+        warm2 = keep.tile([P, 1], F32, name="warm2")
+
+        cell_rows = cell.rearrange("(p t) u -> p t u", t=PACK)
+        out_rows = out_0.rearrange("(p t) s -> p t s", t=PACK)
+        weights = (w1, w2, w3)
+
+        def load_w(i):
+            nc.sync.dma_start(out=w_raw[i][:], in_=weights[i].rearrange("(p j) c -> p j c", j=PACK))
+
+        def load_cell(t):
+            nc.sync.dma_start(out=cell_sb[t][:], in_=cell_rows[:, t, :])
+
+        nc.vector.memset(xs_all[:].bitcast(I32), 0)
+        nc.vector.memset(warm[:], 0.0)
+        nc.sync.dma_start(offs_sb[:], offs)
+        nc.sync.dma_start(out=xw_all[:].bitcast(I32), in_=x_words[0].rearrange("p n t -> p (n t)").bitcast(I32))
+        for q in range(4):
+            nc.sync.dma_start(out=xs_all[32 * q : 32 * q + 4, :].bitcast(I32), in_=x_scales[0, 4 * q : 4 * q + 4, :].bitcast(I32))
+        nc.scalar.activation(warm2[:], warm[:], SIGMOID)
+        nc.sync.dma_start(slot_sb[:], slot)
+        load_cell(0)
+        load_cell(1)
+        load_w(0)
+        load_cell(2)
+        nc.sync.dma_start(out=peep_sb[:], in_=peep.rearrange("(p t) o -> p (t o)", t=PACK))
+        load_w(1)
+        load_cell(3)
+        load_w(2)
+
+        def cast_w(i, h, eng):
+            src = w_raw[i][:].rearrange("p j (m t) -> p m j t", t=PACK)[:, :, :, 2 * h : 2 * h + 2]
+            dst = w_bf[i][:, 2 * h : 2 * h + 2].rearrange("p t m j -> p m j t")
+            if eng == "v":
+                nc.vector.tensor_copy(out=dst, in_=src)
+            else:
+                nc.scalar.copy(out=dst, in_=src)
+
+        def quant_w(i, t0, t1):
+            cols = slice(t0 * P, t1 * P)
+            nc.vector.quantize_mx(out=w_codes[i][:, cols].bitcast(FP8X4), scales=w_scales[i][:, cols], in_=w_bf[i][:, t0:t1].rearrange("p t m j -> p (t m j)"))
+
+        def reuse(i, h):
+            return w_bf[i][:, 2 * h : 2 * h + 2].rearrange("p t m j -> p (t m j)").bitcast(F32)
+
+        pre = [keep.tile([P, S], F32, name="pre%d" % t)[:] for t in range(4)]
+        step = [keep.tile([P, PACK, P], F32, name="step%d" % c)[:] for c in range(2)] + [reuse(2, h).rearrange("p (t s) -> p t s", t=PACK) for h in range(2)]
+
+        def product(i, t, tag, bufs):
+            acc = psum.tile([P, S], F32, name=tag, tag=tag, bufs=bufs)
+            cols = slice(t * P, (t + 1) * P)
+            nc.tensor.matmul_mx(out=acc[:], lhsT=w_codes[i][:, cols].bitcast(FP8X4), lhsT_scale=w_scales[i][:, cols],
+                                rhs=xw[:].bitcast(FP8X4), rhs_scale=xs[:], start=True, stop=True)
+            return acc
+
+        def product_chunk(i, c, tag, bufs):
+            acc = psum.tile([P, PACK, P], F32, name=tag, tag=tag, bufs=bufs)
+            js = slice(c * P, (c + 1) * P)
+            for t in range(PACK):
+                cols = slice(t * P, (t + 1) * P)
+                nc.tensor.matmul_mx(out=acc[:, t, :], lhsT=w_codes[i][:, cols].bitcast(FP8X4), lhsT_scale=w_scales[i][:, cols],
+                                    rhs=xw[:, js].bitcast(FP8X4), rhs_scale=xs[:, js], start=True, stop=True)
+            return acc
+
+        def gather_cell(t):
+            nc.vector.tensor_copy(old[:, t, :], cell_sb[t][:].indirect(slot_sb[:]))
+
+        def forget(t):
+            z1 = product(0, t, "z", 4)
+            nc.vector.scalar_tensor_tensor(out=pre[t], in0=old[:, t, :], scalar=peep_sb[:, t : t + 1], in1=z1[:], op0=MULT, op1=ADD)
+
+        nc.vector.tensor_copy(xw[:], xw_all[:].indirect(offs_sb[:]))
+        nc.vector.tensor_copy(xs[:], xs_all[:].indirect(offs_sb[:]))
+        gather_cell(0)
+        gather_cell(1)
+        cast_w(0, 0, "v")
+        cast_w(0, 1, "s")
+        quant_w(0, 0, 2)
+        quant_w(0, 2, 4)
+        gather_cell(2)
+        forget(0)
+        forget(1)
+        forget(2)
+        cast_w(1, 0, "s")
+        cast_w(1, 1, "s")
+        gather_cell(3)
+        w_codes[1] = keep.tile([P, N], U32, name="w_codes1", tag="cell3", align_bytes=64)
+        quant_w(1, 0, 2)
+        quant_w(1, 2, 4)
+        forget(3)
+        for t in range(PACK):
+            nc.scalar.activation(fg[:, t, :], pre[t], SIGMOID)
+        cast_w(2, 0, "s")
+        cast_w(2, 1, "s")
+        y = [product_chunk(1, c, "y", 4) for c in range(4)]
+        for c in range(4):
+            nc.vector.tensor_tensor(diff[c][:], old[:, :, c * P : (c + 1) * P], y[c][:], SUB)
+        quant_w(2, 0, 4)
+        for c in range(4):
+            z3 = product_chunk(2, c, "z", 4)
+            nc.scalar.activation(rg[c][:], z3[:], SIGMOID)
+            nc.vector.tensor_tensor(step[c], fg[:, :, c * P : (c + 1) * P], diff[c][:], MULT)
+        words_out = out_1[0].rearrange("p n t -> p (n t)").bitcast(I32)
+
+        def gate(c):
+            nc.vector.tensor_tensor(gated[c][:], step[c], rg[c][:], MULT)
+
+        def finish(c):
+            nc.vector.tensor_tensor(res[c][:], gated[c][:], y[c][:], ADD)
+            nc.sync.dma_start(out=out_rows[:, :, c * P : (c + 1) * P], in_=res[c][:])
+            src = res[c][:].rearrange("p t (c i) -> p c t i", i=4)
+            dst = res_bf[c][:].rearrange("p (c i) t -> p c t i", i=4)
+            nc.scalar.copy(out=dst, in_=src)
+
+        def quant_res(c):
+            js = slice(c * P, (c + 1) * P)
+            nc.vector.quantize_mx(out=res_codes[:, js].bitcast(FP8X4), scales=res_scales[:, js], in_=res_bf[c][:].rearrange("p s t -> p (s t)"))
+
+        gate(0)
+        gate(1)
+        finish(0)
+        gate(2)
+        finish(1)
+        gate(3)
+        finish(2)
+        quant_res(0)
+        finish(3)
+        quant_res(1)
+        quant_res(2)
+        nc.sync.dma_start(out=words_out[:, 0 : 3 * P], in_=res_codes[:, 0 : 3 * P].bitcast(I32))
+        quant_res(3)
+        nc.sync.dma_start(out=words_out[:, 3 * P : S], in_=res_codes[:, 3 * P : S].bitcast(I32))
+        for q in range(4):
+            eng = nc.scalar if q % 2 else nc.sync
+            eng.dma_start(out=out_2[0, 4 * q : 4 * q + 4, :].bitcast(I32), in_=res_scales[32 * q : 32 * q + 4, :].bitcast(I32))

@@ -19,6 +19,7 @@ SIGMOID = mybir.ActivationFunctionType.Sigmoid
 
 P = 128
 PACK = 4
+H = S // 2
 
 
 def tile_picked_ysru_hwy_po_kernel(tc, x_words, x_scales, cell, w1, w2, w3, peep, offs, slot, out_0, out_1, out_2):
@@ -29,23 +30,24 @@ def tile_picked_ysru_hwy_po_kernel(tc, x_words, x_scales, cell, w1, w2, w3, peep
 
         offs_sb = keep.tile([P, S // 16], U16, name="offs_sb")
         slot_sb = keep.tile([P, S // 16], U16, name="slot_sb")
-        peep_sb = keep.tile([P, PACK], F32, name="peep_sb")
+        peep_sb = [keep.tile([P, 2], F32, name="peep%d" % h) for h in range(2)]
         xw_all = keep.tile([P, T], U32, name="xw_all")
         xs_all = keep.tile([P, T], U8, name="xs_all")
         xw = keep.tile([P, S], U32, name="xw", align_bytes=64)
         xs = keep.tile([P, S], U8, name="xs", align_bytes=64)
         cell_sb = [keep.tile([P, U], F32, name="cell%d" % t, tag="cell%d" % t, align_bytes=64) for t in range(PACK)]
         w_raw = [keep.tile([P, PACK, N], F32, name="w_raw%d" % i) for i in range(3)]
-        w_bf = [keep.tile([P, PACK, P, PACK], BF16, name="w_bf%d" % i, align_bytes=64) for i in range(3)]
-        w_codes = {i: keep.tile([P, N], U32, name="w_codes%d" % i, align_bytes=64) for i in (0, 2)}
-        w_scales = [keep.tile([P, N], U8, name="w_scales%d" % i, align_bytes=64) for i in range(3)]
+        w_bf = [[keep.tile([P, 2, P, PACK], BF16, name="w_bf%d_%d" % (i, h), align_bytes=64) for h in range(2)] for i in range(3)]
+        w_codes = {}
+        w_scales = [[keep.tile([P, 2 * P], U8, name="w_scales%d_%d" % (i, h), align_bytes=64) for h in range(2)] for i in range(3)]
         old = keep.tile([P, PACK, S], F32, name="old")
+        pre = keep.tile([P, PACK, S], F32, name="pre")
         fg = w_raw[1]
-        rg = [keep.tile([P, PACK, P], F32, name="rg%d" % c) for c in range(4)]
-        diff = [keep.tile([P, PACK, P], F32, name="diff%d" % c) for c in range(4)]
-        gated = [keep.tile([P, PACK, P], F32, name="gated%d" % c) for c in range(4)]
-        res = [keep.tile([P, PACK, P], F32, name="res%d" % c) for c in range(4)]
-        res_bf = [keep.tile([P, P, PACK], BF16, name="res_bf%d" % c, align_bytes=64) for c in range(4)]
+        rg = [keep.tile([P, S], F32, name="rg%d" % u) for u in range(4)]
+        diff = [keep.tile([P, S], F32, name="diff%d" % u) for u in range(4)]
+        step = [w_bf[2][0][:].rearrange("p t m j -> p (t m j)").bitcast(F32)] + [keep.tile([P, S], F32, name="step%d" % u)[:] for u in range(1, 4)]
+        gated = [keep.tile([P, S], F32, name="gated%d" % u) for u in range(4)]
+        res_bf = keep.tile([P, S, PACK], BF16, name="res_bf", align_bytes=64)
         res_codes = keep.tile([P, S], U32, name="res_codes", align_bytes=64)
         res_scales = keep.tile([P, S], U8, name="res_scales", align_bytes=64)
         warm = keep.tile([P, 1], F32, name="warm")
@@ -53,6 +55,7 @@ def tile_picked_ysru_hwy_po_kernel(tc, x_words, x_scales, cell, w1, w2, w3, peep
 
         cell_rows = cell.rearrange("(p t) u -> p t u", t=PACK)
         out_rows = out_0.rearrange("(p t) s -> p t s", t=PACK)
+        peep_rows = peep.rearrange("(p t) o -> p (t o)", t=PACK)
         weights = (w1, w2, w3)
 
         def load_w(i):
@@ -72,52 +75,77 @@ def tile_picked_ysru_hwy_po_kernel(tc, x_words, x_scales, cell, w1, w2, w3, peep
         load_cell(0)
         load_cell(1)
         load_w(0)
-        load_cell(2)
-        nc.sync.dma_start(out=peep_sb[:], in_=peep.rearrange("(p t) o -> p (t o)", t=PACK))
+        nc.sync.dma_start(out=peep_sb[0][:], in_=peep_rows[:, 0:2])
         load_w(1)
-        load_cell(3)
         load_w(2)
+        load_cell(2)
+        load_cell(3)
+        nc.sync.dma_start(out=peep_sb[1][:], in_=peep_rows[:, 2:4])
 
         def cast_w(i, h, eng):
             src = w_raw[i][:].rearrange("p j (m t) -> p m j t", t=PACK)[:, :, :, 2 * h : 2 * h + 2]
-            dst = w_bf[i][:, 2 * h : 2 * h + 2].rearrange("p t m j -> p m j t")
+            dst = w_bf[i][h][:].rearrange("p t m j -> p m j t")
             if eng == "v":
                 nc.vector.tensor_copy(out=dst, in_=src)
             else:
                 nc.scalar.copy(out=dst, in_=src)
 
-        def quant_w(i, t0, t1):
-            cols = slice(t0 * P, t1 * P)
-            nc.vector.quantize_mx(out=w_codes[i][:, cols].bitcast(FP8X4), scales=w_scales[i][:, cols], in_=w_bf[i][:, t0:t1].rearrange("p t m j -> p (t m j)"))
+        def quant_w(i, h, tag):
+            w_codes[i, h] = keep.tile([P, 2 * P], U32, name=tag, tag=tag, align_bytes=64)
+            nc.vector.quantize_mx(out=w_codes[i, h][:].bitcast(FP8X4), scales=w_scales[i][h][:], in_=w_bf[i][h][:].rearrange("p t m j -> p (t m j)"))
 
-        def reuse(i, h):
-            return w_bf[i][:, 2 * h : 2 * h + 2].rearrange("p t m j -> p (t m j)").bitcast(F32)
+        def mm(dst, i, t, js):
+            cols = slice((t % 2) * P, (t % 2 + 1) * P)
+            nc.tensor.matmul_mx(out=dst, lhsT=w_codes[i, t // 2][:, cols].bitcast(FP8X4), lhsT_scale=w_scales[i][t // 2][:, cols],
+                                rhs=xw[:, js].bitcast(FP8X4), rhs_scale=xs[:, js], start=True, stop=True)
 
-        pre = [keep.tile([P, S], F32, name="pre%d" % t)[:] for t in range(4)]
-        step = [keep.tile([P, PACK, P], F32, name="step%d" % c)[:] for c in range(2)] + [reuse(2, h).rearrange("p (t s) -> p t s", t=PACK) for h in range(2)]
-
-        def product(i, t, tag, bufs):
-            acc = psum.tile([P, S], F32, name=tag, tag=tag, bufs=bufs)
-            cols = slice(t * P, (t + 1) * P)
-            nc.tensor.matmul_mx(out=acc[:], lhsT=w_codes[i][:, cols].bitcast(FP8X4), lhsT_scale=w_scales[i][:, cols],
-                                rhs=xw[:].bitcast(FP8X4), rhs_scale=xs[:], start=True, stop=True)
+        def plane_product(i, t, tag):
+            acc = psum.tile([P, S], F32, name=tag, tag=tag, bufs=4)
+            mm(acc[:], i, t, slice(0, S))
             return acc
 
-        def product_chunk(i, c, tag, bufs):
-            acc = psum.tile([P, PACK, P], F32, name=tag, tag=tag, bufs=bufs)
-            js = slice(c * P, (c + 1) * P)
-            for t in range(PACK):
-                cols = slice(t * P, (t + 1) * P)
-                nc.tensor.matmul_mx(out=acc[:, t, :], lhsT=w_codes[i][:, cols].bitcast(FP8X4), lhsT_scale=w_scales[i][:, cols],
-                                    rhs=xw[:, js].bitcast(FP8X4), rhs_scale=xs[:, js], start=True, stop=True)
+        def product(i, u, tag):
+            if u < 2:
+                return plane_product(i, u, tag)
+            acc = psum.tile([P, S], F32, name=tag, tag=tag, bufs=4)
+            for t in (2, 3):
+                mm(acc[:, (t - 2) * H : (t - 1) * H], i, t, slice((u - 2) * H, (u - 1) * H))
             return acc
+
+        def unit(tile4, u):
+            if u < 2:
+                return tile4[:, u, :]
+            return tile4[:, 2:4, (u - 2) * H : (u - 1) * H]
+
+        def shaped(flat, u):
+            if u < 2:
+                return flat
+            return flat.rearrange("p (t s) -> p t s", t=2)
 
         def gather_cell(t):
             nc.vector.tensor_copy(old[:, t, :], cell_sb[t][:].indirect(slot_sb[:]))
 
+        z1 = {}
+        y = {}
+
         def forget(t):
-            z1 = product(0, t, "z", 4)
-            nc.vector.scalar_tensor_tensor(out=pre[t], in0=old[:, t, :], scalar=peep_sb[:, t : t + 1], in1=z1[:], op0=MULT, op1=ADD)
+            nc.vector.scalar_tensor_tensor(out=pre[:, t, :], in0=old[:, t, :], scalar=peep_sb[t // 2][:, t % 2 : t % 2 + 1], in1=z1[t][:], op0=MULT, op1=ADD)
+
+        def forget_gate(t):
+            nc.scalar.activation(fg[:, t, :], pre[:, t, :], SIGMOID)
+
+        def reset_gate(u):
+            z3 = product(2, u, "z")
+            nc.scalar.activation(rg[u][:], z3[:], SIGMOID)
+
+        def difference(u):
+            nc.vector.tensor_tensor(shaped(diff[u][:], u), unit(old, u), shaped(y[u][:], u), SUB)
+
+        def stepped(u, eng):
+            eng.tensor_tensor(shaped(step[u], u), unit(fg, u), shaped(diff[u][:], u), MULT)
+
+        def gate(u, eng):
+            eng.tensor_tensor(gated[u][:], step[u], rg[u][:], MULT)
 
         nc.vector.tensor_copy(xw[:], xw_all[:].indirect(offs_sb[:]))
         nc.vector.tensor_copy(xs[:], xs_all[:].indirect(offs_sb[:]))
@@ -125,61 +153,79 @@ def tile_picked_ysru_hwy_po_kernel(tc, x_words, x_scales, cell, w1, w2, w3, peep
         gather_cell(1)
         cast_w(0, 0, "v")
         cast_w(0, 1, "s")
-        quant_w(0, 0, 2)
-        quant_w(0, 2, 4)
-        gather_cell(2)
+        quant_w(0, 0, "w1a")
+        quant_w(0, 1, "w1b")
+        for t in range(PACK):
+            z1[t] = plane_product(0, t, "z")
         forget(0)
         forget(1)
-        forget(2)
-        cast_w(1, 0, "s")
+        cast_w(1, 0, "v")
         cast_w(1, 1, "s")
-        gather_cell(3)
-        w_codes[1] = keep.tile([P, N], U32, name="w_codes1", tag="cell3", align_bytes=64)
-        quant_w(1, 0, 2)
-        quant_w(1, 2, 4)
-        forget(3)
-        for t in range(PACK):
-            nc.scalar.activation(fg[:, t, :], pre[t], SIGMOID)
+        quant_w(1, 0, "w2a")
+        quant_w(1, 1, "w2b")
+        forget_gate(0)
+        forget_gate(1)
+        for u in range(4):
+            y[u] = product(1, u, "y")
+        difference(0)
+        difference(1)
         cast_w(2, 0, "s")
         cast_w(2, 1, "s")
-        y = [product_chunk(1, c, "y", 4) for c in range(4)]
-        for c in range(4):
-            nc.vector.tensor_tensor(diff[c][:], old[:, :, c * P : (c + 1) * P], y[c][:], SUB)
-        quant_w(2, 0, 4)
-        for c in range(4):
-            z3 = product_chunk(2, c, "z", 4)
-            nc.scalar.activation(rg[c][:], z3[:], SIGMOID)
-            nc.vector.tensor_tensor(step[c], fg[:, :, c * P : (c + 1) * P], diff[c][:], MULT)
+        quant_w(2, 0, "w3a")
+        stepped(0, nc.gpsimd)
+        stepped(1, nc.gpsimd)
+        reset_gate(0)
+        reset_gate(1)
+        gather_cell(2)
+        gather_cell(3)
+        quant_w(2, 1, "cell3")
+        gate(0, nc.gpsimd)
+        gate(1, nc.gpsimd)
+        forget(2)
+        forget_gate(2)
+        forget(3)
+        forget_gate(3)
+        reset_gate(2)
+        reset_gate(3)
+        difference(2)
+        difference(3)
+        stepped(2, nc.gpsimd)
+        res = keep.tile([P, PACK, S], F32, name="res", tag="cell3", align_bytes=64)
+        for u in range(2):
+            nc.vector.tensor_tensor(res[:, u, :], gated[u][:], y[u][:], ADD)
+            nc.sync.dma_start(out=out_rows[:, u, :], in_=res[:, u, :])
+
+        def finish(u, a, b):
+            j0 = (u - 2) * H
+            nc.vector.tensor_tensor(res[:, 2:4, j0 + a : j0 + b], shaped(gated[u][:], u)[:, :, a:b], shaped(y[u][:], u)[:, :, a:b], ADD)
+
+        def round_res(a, b, eng):
+            src = res[:, :, a:b].rearrange("p t (c i) -> p c t i", i=4)
+            dst = res_bf[:, a:b, :].rearrange("p (c i) t -> p c t i", i=4)
+            if eng == "v":
+                nc.vector.tensor_copy(out=dst, in_=src)
+            else:
+                nc.scalar.copy(out=dst, in_=src)
+
         words_out = out_1[0].rearrange("p n t -> p (n t)").bitcast(I32)
 
-        def gate(c):
-            nc.vector.tensor_tensor(gated[c][:], step[c], rg[c][:], MULT)
+        def quant_res(a, b):
+            nc.vector.quantize_mx(out=res_codes[:, a:b].bitcast(FP8X4), scales=res_scales[:, a:b], in_=res_bf[:, a:b, :].rearrange("p s t -> p (s t)"))
+            nc.sync.dma_start(out=words_out[:, a:b], in_=res_codes[:, a:b].bitcast(I32))
 
-        def finish(c):
-            nc.vector.tensor_tensor(res[c][:], gated[c][:], y[c][:], ADD)
-            nc.sync.dma_start(out=out_rows[:, :, c * P : (c + 1) * P], in_=res[c][:])
-            src = res[c][:].rearrange("p t (c i) -> p c t i", i=4)
-            dst = res_bf[c][:].rearrange("p (c i) t -> p c t i", i=4)
-            nc.scalar.copy(out=dst, in_=src)
-
-        def quant_res(c):
-            js = slice(c * P, (c + 1) * P)
-            nc.vector.quantize_mx(out=res_codes[:, js].bitcast(FP8X4), scales=res_scales[:, js], in_=res_bf[c][:].rearrange("p s t -> p (s t)"))
-
-        gate(0)
-        gate(1)
-        finish(0)
-        gate(2)
-        finish(1)
-        gate(3)
-        finish(2)
-        quant_res(0)
-        finish(3)
-        quant_res(1)
-        quant_res(2)
-        nc.sync.dma_start(out=words_out[:, 0 : 3 * P], in_=res_codes[:, 0 : 3 * P].bitcast(I32))
-        quant_res(3)
-        nc.sync.dma_start(out=words_out[:, 3 * P : S], in_=res_codes[:, 3 * P : S].bitcast(I32))
+        gate(2, nc.vector)
+        stepped(3, nc.vector)
+        finish(2, 0, H)
+        nc.sync.dma_start(out=out_rows[:, 2:4, 0:H], in_=res[:, 2:4, 0:H])
+        round_res(0, H, "s")
+        gate(3, nc.vector)
+        finish(3, 0, P)
+        round_res(H, H + P, "s")
+        finish(3, P, H)
+        nc.sync.dma_start(out=out_rows[:, 2:4, H:S], in_=res[:, 2:4, H:S])
+        quant_res(0, H)
+        round_res(H + P, S, "v")
+        quant_res(H, S)
         for q in range(4):
             eng = nc.scalar if q % 2 else nc.sync
             eng.dma_start(out=out_2[0, 4 * q : 4 * q + 4, :].bitcast(I32), in_=res_scales[32 * q : 32 * q + 4, :].bitcast(I32))

@@ -28,25 +28,33 @@ def tile_picked_ysru_hwy_po_kernel(tc, x_words, x_scales, cell, w1, w2, w3, peep
         keep = ctx.enter_context(tc.tile_pool(name="keep", bufs=1))
         psum = ctx.enter_context(tc.psum_pool(name="psum", bufs=1))
 
+        after_cell3 = ctx.enter_context(tc.tile_pool(name="after_cell3", bufs=1))
+        after_w3 = ctx.enter_context(tc.tile_pool(name="after_w3", bufs=1))
+
         offs_sb = keep.tile([P, S // 16], U16, name="offs_sb")
         slot_sb = keep.tile([P, S // 16], U16, name="slot_sb")
-        peep_sb = [keep.tile([P, 2], F32, name="peep%d" % h) for h in range(2)]
+        peep_sb = keep.tile([P, PACK], F32, name="peep_sb")
         xw_all = keep.tile([P, T], U32, name="xw_all")
         xs_all = keep.tile([P, T], U8, name="xs_all")
         xw = keep.tile([P, S], U32, name="xw", align_bytes=64)
         xs = keep.tile([P, S], U8, name="xs", align_bytes=64)
-        cell_sb = [keep.tile([P, U], F32, name="cell%d" % t, tag="cell%d" % t, align_bytes=64) for t in range(PACK)]
+        cell_sb = [keep.tile([P, U], F32, name="cell%d" % t) for t in range(3)]
+        cell_sb.append(after_cell3.tile([P, U], F32, name="cell3", offset=0, align_bytes=64))
         w_raw = [keep.tile([P, PACK, N], F32, name="w_raw%d" % i) for i in range(3)]
-        w_bf = [[keep.tile([P, 2, P, PACK], BF16, name="w_bf%d_%d" % (i, h), align_bytes=64) for h in range(2)] for i in range(3)]
-        w_codes = {}
+        w_bf = [[keep.tile([P, 2, P, PACK], BF16, name="w_bf%d_%d" % (i, h), align_bytes=64) for h in range(2)] for i in range(2)]
+        w_bf.append([after_w3.tile([P, 2, P, PACK], BF16, name="w_bf2_%d" % h, offset=2048 * h, align_bytes=64) for h in range(2)])
+        w_codes = {(i, h): keep.tile([P, 2 * P], U32, name="w_codes%d_%d" % (i, h), align_bytes=64) for i in range(3) for h in range(2) if (i, h) != (1, 1)}
+        w_codes[1, 1] = after_cell3.tile([P, 2 * P], U32, name="w_codes1_1", offset=2048, align_bytes=64)
         w_scales = [[keep.tile([P, 2 * P], U8, name="w_scales%d_%d" % (i, h), align_bytes=64) for h in range(2)] for i in range(3)]
         old = keep.tile([P, PACK, S], F32, name="old")
         pre = keep.tile([P, PACK, S], F32, name="pre")
         fg = w_raw[1]
-        rg = [keep.tile([P, S], F32, name="rg%d" % u) for u in range(4)]
-        diff = [keep.tile([P, S], F32, name="diff%d" % u) for u in range(4)]
-        step = [w_bf[2][0][:].rearrange("p t m j -> p (t m j)").bitcast(F32)] + [keep.tile([P, S], F32, name="step%d" % u)[:] for u in range(1, 4)]
-        gated = [keep.tile([P, S], F32, name="gated%d" % u) for u in range(4)]
+        rg = [keep.tile([P, 2, H], F32, name="rg%d" % u) for u in range(4)]
+        diff = [after_cell3.tile([P, 2, H], F32, name="diff0", offset=0, align_bytes=64)] + [keep.tile([P, 2, H], F32, name="diff%d" % u) for u in range(1, 4)]
+        step = [keep.tile([P, 2, H], F32, name="step%d" % u) for u in range(2)]
+        step.extend([after_w3.tile([P, 2, H], F32, name="step%d" % u, offset=1024 + 2048 * (u - 2), align_bytes=64) for u in (2, 3)])
+        gated = [step[2] if u == 1 else keep.tile([P, 2, H], F32, name="gated%d" % u) for u in range(4)]
+        res = keep.tile([P, PACK, S], F32, name="res")
         res_bf = keep.tile([P, S, PACK], BF16, name="res_bf", align_bytes=64)
         res_codes = keep.tile([P, S], U32, name="res_codes", align_bytes=64)
         res_scales = keep.tile([P, S], U8, name="res_scales", align_bytes=64)
@@ -55,7 +63,7 @@ def tile_picked_ysru_hwy_po_kernel(tc, x_words, x_scales, cell, w1, w2, w3, peep
 
         cell_rows = cell.rearrange("(p t) u -> p t u", t=PACK)
         out_rows = out_0.rearrange("(p t) s -> p t s", t=PACK)
-        peep_rows = peep.rearrange("(p t) o -> p (t o)", t=PACK)
+        words_out = out_1[0].rearrange("p n t -> p (n t)").bitcast(I32)
         weights = (w1, w2, w3)
 
         def load_w(i):
@@ -75,23 +83,17 @@ def tile_picked_ysru_hwy_po_kernel(tc, x_words, x_scales, cell, w1, w2, w3, peep
         load_cell(0)
         load_cell(1)
         load_w(0)
-        nc.sync.dma_start(out=peep_sb[0][:], in_=peep_rows[:, 0:2])
-        load_w(1)
-        load_w(2)
         load_cell(2)
+        nc.sync.dma_start(out=peep_sb[:], in_=peep.rearrange("(p t) o -> p (t o)", t=PACK))
+        load_w(1)
         load_cell(3)
-        nc.sync.dma_start(out=peep_sb[1][:], in_=peep_rows[:, 2:4])
+        load_w(2)
 
-        def cast_w(i, h, eng):
+        def cast_w(i, h, copy):
             src = w_raw[i][:].rearrange("p j (m t) -> p m j t", t=PACK)[:, :, :, 2 * h : 2 * h + 2]
-            dst = w_bf[i][h][:].rearrange("p t m j -> p m j t")
-            if eng == "v":
-                nc.vector.tensor_copy(out=dst, in_=src)
-            else:
-                nc.scalar.copy(out=dst, in_=src)
+            copy(out=w_bf[i][h][:].rearrange("p t m j -> p m j t"), in_=src)
 
-        def quant_w(i, h, tag):
-            w_codes[i, h] = keep.tile([P, 2 * P], U32, name=tag, tag=tag, align_bytes=64)
+        def quant_w(i, h):
             nc.vector.quantize_mx(out=w_codes[i, h][:].bitcast(FP8X4), scales=w_scales[i][h][:], in_=w_bf[i][h][:].rearrange("p t m j -> p (t m j)"))
 
         def mm(dst, i, t, js):
@@ -99,37 +101,22 @@ def tile_picked_ysru_hwy_po_kernel(tc, x_words, x_scales, cell, w1, w2, w3, peep
             nc.tensor.matmul_mx(out=dst, lhsT=w_codes[i, t // 2][:, cols].bitcast(FP8X4), lhsT_scale=w_scales[i][t // 2][:, cols],
                                 rhs=xw[:, js].bitcast(FP8X4), rhs_scale=xs[:, js], start=True, stop=True)
 
-        def plane_product(i, t, tag):
-            acc = psum.tile([P, S], F32, name=tag, tag=tag, bufs=4)
-            mm(acc[:], i, t, slice(0, S))
-            return acc
-
         def product(i, u, tag):
-            if u < 2:
-                return plane_product(i, u, tag)
-            acc = psum.tile([P, S], F32, name=tag, tag=tag, bufs=4)
-            for t in (2, 3):
-                mm(acc[:, (t - 2) * H : (t - 1) * H], i, t, slice((u - 2) * H, (u - 1) * H))
+            acc = psum.tile([P, 2, H], F32, name=tag, tag=tag, bufs=4)
+            for k in range(2):
+                mm(acc[:, k, :], i, 2 * (u // 2) + k, slice((u % 2) * H, (u % 2 + 1) * H))
             return acc
 
-        def unit(tile4, u):
-            if u < 2:
-                return tile4[:, u, :]
-            return tile4[:, 2:4, (u - 2) * H : (u - 1) * H]
-
-        def shaped(flat, u):
-            if u < 2:
-                return flat
-            return flat.rearrange("p (t s) -> p t s", t=2)
+        def unit(tile4, u, a=0, b=H):
+            return tile4[:, 2 * (u // 2) : 2 * (u // 2) + 2, (u % 2) * H + a : (u % 2) * H + b]
 
         def gather_cell(t):
             nc.vector.tensor_copy(old[:, t, :], cell_sb[t][:].indirect(slot_sb[:]))
 
-        z1 = {}
-        y = {}
-
         def forget(t):
-            nc.vector.scalar_tensor_tensor(out=pre[:, t, :], in0=old[:, t, :], scalar=peep_sb[t // 2][:, t % 2 : t % 2 + 1], in1=z1[t][:], op0=MULT, op1=ADD)
+            z1 = psum.tile([P, S], F32, name="z", tag="z", bufs=4)
+            mm(z1[:], 0, t, slice(0, S))
+            nc.vector.scalar_tensor_tensor(out=pre[:, t, :], in0=old[:, t, :], scalar=peep_sb[:, t : t + 1], in1=z1[:], op0=MULT, op1=ADD)
 
         def forget_gate(t):
             nc.scalar.activation(fg[:, t, :], pre[:, t, :], SIGMOID)
@@ -138,94 +125,83 @@ def tile_picked_ysru_hwy_po_kernel(tc, x_words, x_scales, cell, w1, w2, w3, peep
             z3 = product(2, u, "z")
             nc.scalar.activation(rg[u][:], z3[:], SIGMOID)
 
+        y = {}
+
         def difference(u):
-            nc.vector.tensor_tensor(shaped(diff[u][:], u), unit(old, u), shaped(y[u][:], u), SUB)
+            nc.vector.tensor_tensor(diff[u][:], unit(old, u), y[u][:], SUB)
 
         def stepped(u, eng):
-            eng.tensor_tensor(shaped(step[u], u), unit(fg, u), shaped(diff[u][:], u), MULT)
+            eng.tensor_tensor(step[u][:], unit(fg, u), diff[u][:], MULT)
 
         def gate(u, eng):
-            eng.tensor_tensor(gated[u][:], step[u], rg[u][:], MULT)
+            eng.tensor_tensor(gated[u][:], step[u][:], rg[u][:], MULT)
+
+        def finish(u, a, b):
+            nc.vector.tensor_tensor(unit(res, u, a, b), gated[u][:, :, a:b], y[u][:, :, a:b], ADD)
+
+        def round_res(a, b, copy):
+            copy(out=res_bf[:, a:b, :].rearrange("p (c i) t -> p c t i", i=4), in_=res[:, :, a:b].rearrange("p t (c i) -> p c t i", i=4))
+
+        def quant_res(a, b):
+            nc.vector.quantize_mx(out=res_codes[:, a:b].bitcast(FP8X4), scales=res_scales[:, a:b], in_=res_bf[:, a:b, :].rearrange("p s t -> p (s t)"))
 
         nc.vector.tensor_copy(xw[:], xw_all[:].indirect(offs_sb[:]))
         nc.vector.tensor_copy(xs[:], xs_all[:].indirect(offs_sb[:]))
         gather_cell(0)
         gather_cell(1)
-        cast_w(0, 0, "v")
-        cast_w(0, 1, "s")
-        quant_w(0, 0, "w1a")
-        quant_w(0, 1, "w1b")
-        for t in range(PACK):
-            z1[t] = plane_product(0, t, "z")
-        forget(0)
-        forget(1)
-        cast_w(1, 0, "v")
-        cast_w(1, 1, "s")
-        quant_w(1, 0, "w2a")
-        quant_w(1, 1, "w2b")
-        forget_gate(0)
-        forget_gate(1)
+        cast_w(0, 0, nc.vector.tensor_copy)
+        cast_w(0, 1, nc.scalar.copy)
+        quant_w(0, 0)
+        quant_w(0, 1)
+        gather_cell(2)
+        for t in range(3):
+            forget(t)
+        cast_w(1, 0, nc.scalar.copy)
+        cast_w(1, 1, nc.scalar.copy)
+        quant_w(1, 0)
+        gather_cell(3)
+        quant_w(1, 1)
         for u in range(4):
             y[u] = product(1, u, "y")
+        for t in range(3):
+            forget_gate(t)
         difference(0)
-        difference(1)
-        cast_w(2, 0, "s")
-        cast_w(2, 1, "s")
-        quant_w(2, 0, "w3a")
         stepped(0, nc.gpsimd)
-        stepped(1, nc.gpsimd)
-        reset_gate(0)
-        reset_gate(1)
-        gather_cell(2)
-        gather_cell(3)
-        quant_w(2, 1, "cell3")
-        gate(0, nc.gpsimd)
-        gate(1, nc.gpsimd)
-        forget(2)
-        forget_gate(2)
         forget(3)
+        difference(1)
+        stepped(1, nc.gpsimd)
+        cast_w(2, 0, nc.scalar.copy)
         forget_gate(3)
-        reset_gate(2)
-        reset_gate(3)
+        cast_w(2, 1, nc.scalar.copy)
         difference(2)
         difference(3)
-        stepped(2, nc.gpsimd)
-        res = keep.tile([P, PACK, S], F32, name="res", tag="cell3", align_bytes=64)
-        for u in range(2):
-            nc.vector.tensor_tensor(res[:, u, :], gated[u][:], y[u][:], ADD)
-            nc.sync.dma_start(out=out_rows[:, u, :], in_=res[:, u, :])
-
-        def finish(u, a, b):
-            j0 = (u - 2) * H
-            nc.vector.tensor_tensor(res[:, 2:4, j0 + a : j0 + b], shaped(gated[u][:], u)[:, :, a:b], shaped(y[u][:], u)[:, :, a:b], ADD)
-
-        def round_res(a, b, eng):
-            src = res[:, :, a:b].rearrange("p t (c i) -> p c t i", i=4)
-            dst = res_bf[:, a:b, :].rearrange("p (c i) t -> p c t i", i=4)
-            if eng == "v":
-                nc.vector.tensor_copy(out=dst, in_=src)
-            else:
-                nc.scalar.copy(out=dst, in_=src)
-
-        words_out = out_1[0].rearrange("p n t -> p (n t)").bitcast(I32)
-
-        def quant_res(a, b):
-            nc.vector.quantize_mx(out=res_codes[:, a:b].bitcast(FP8X4), scales=res_scales[:, a:b], in_=res_bf[:, a:b, :].rearrange("p s t -> p (s t)"))
-            nc.sync.dma_start(out=words_out[:, a:b], in_=res_codes[:, a:b].bitcast(I32))
-
-        gate(2, nc.vector)
+        quant_w(2, 0)
+        quant_w(2, 1)
+        for u in (0, 2, 1, 3):
+            reset_gate(u)
+        stepped(2, nc.vector)
         stepped(3, nc.vector)
+        gate(0, nc.vector)
+        gate(2, nc.vector)
+        gate(1, nc.gpsimd)
+        finish(0, 0, H)
         finish(2, 0, H)
-        nc.sync.dma_start(out=out_rows[:, 2:4, 0:H], in_=res[:, 2:4, 0:H])
-        round_res(0, H, "s")
+        nc.sync.dma_start(out=out_rows[:, :, 0:H], in_=res[:, :, 0:H])
+        round_res(0, H, nc.scalar.copy)
         gate(3, nc.vector)
+        finish(1, 0, P)
         finish(3, 0, P)
-        round_res(H, H + P, "s")
+        nc.sync.dma_start(out=out_rows[:, :, H : H + P], in_=res[:, :, H : H + P])
+        round_res(H, H + P, nc.scalar.copy)
+        finish(1, P, H)
         finish(3, P, H)
-        nc.sync.dma_start(out=out_rows[:, 2:4, H:S], in_=res[:, 2:4, H:S])
+        nc.sync.dma_start(out=out_rows[:, :, H + P : S], in_=res[:, :, H + P : S])
         quant_res(0, H)
-        round_res(H + P, S, "v")
-        quant_res(H, S)
+        nc.sync.dma_start(out=words_out[:, 0:H], in_=res_codes[:, 0:H].bitcast(I32))
+        round_res(H + P, S, nc.vector.tensor_copy)
+        quant_res(H, H + P)
+        quant_res(H + P, S)
+        nc.sync.dma_start(out=words_out[:, H:S], in_=res_codes[:, H:S].bitcast(I32))
         for q in range(4):
             eng = nc.scalar if q % 2 else nc.sync
             eng.dma_start(out=out_2[0, 4 * q : 4 * q + 4, :].bitcast(I32), in_=res_scales[32 * q : 32 * q + 4, :].bitcast(I32))

from contextlib import ExitStack

import concourse.mybir as mybir

K, T, S, N, U = 512, 1024, 512, 512, 1024
FLOPS = 3 * 2 * K * N * S

F32 = mybir.dt.float32
BF16 = mybir.dt.bfloat16
I32 = mybir.dt.int32
U32 = mybir.dt.uint32
U16 = mybir.dt.uint16
U8 = mybir.dt.uint8
FP8X4 = mybir.dt.float8_e4m3fn_x4
MULT = mybir.AluOpType.mult
ADD = mybir.AluOpType.add
SUB = mybir.AluOpType.subtract
SIGMOID = mybir.ActivationFunctionType.Sigmoid

P = 128
PACK = 4
H = S // 2


def tile_picked_ysru_hwy_po_kernel(tc, x_words, x_scales, cell, w1, w2, w3, peep, offs, slot, out_0, out_1, out_2):
    nc = tc.nc
    with ExitStack() as ctx:
        keep = ctx.enter_context(tc.tile_pool(name="keep", bufs=1))
        psum = ctx.enter_context(tc.psum_pool(name="psum", bufs=1))

        after_cell3 = ctx.enter_context(tc.tile_pool(name="after_cell3", bufs=1))
        after_w3 = ctx.enter_context(tc.tile_pool(name="after_w3", bufs=1))

        offs_sb = keep.tile([P, S // 16], U16, name="offs_sb")
        slot_sb = keep.tile([P, S // 16], U16, name="slot_sb")
        peep_sb = keep.tile([P, PACK], F32, name="peep_sb")
        xw_all = keep.tile([P, T], U32, name="xw_all")
        xs_all = keep.tile([P, T], U8, name="xs_all")
        xw = keep.tile([P, S], U32, name="xw", align_bytes=64)
        xs = keep.tile([P, S], U8, name="xs", align_bytes=64)
        cell_sb = [keep.tile([P, U], F32, name="cell%d" % t) for t in range(3)]
        cell_sb.append(after_cell3.tile([P, U], F32, name="cell3", offset=0, align_bytes=64))
        w_raw = [keep.tile([P, PACK, N], F32, name="w_raw%d" % i) for i in range(3)]
        w_bf = [[keep.tile([P, 2, P, PACK], BF16, name="w_bf%d_%d" % (i, h), align_bytes=64) for h in range(2)] for i in range(2)]
        w_bf.append([after_w3.tile([P, 2, P, PACK], BF16, name="w_bf2_%d" % h, offset=2048 * h, align_bytes=64) for h in range(2)])
        w_codes = {(i, h): keep.tile([P, 2 * P], U32, name="w_codes%d_%d" % (i, h), align_bytes=64) for i in range(3) for h in range(2) if (i, h) != (1, 1)}
        w_codes[1, 1] = after_cell3.tile([P, 2 * P], U32, name="w_codes1_1", offset=2048, align_bytes=64)
        w_scales = [[keep.tile([P, 2 * P], U8, name="w_scales%d_%d" % (i, h), align_bytes=64) for h in range(2)] for i in range(3)]
        old = keep.tile([P, PACK, S], F32, name="old")
        pre = keep.tile([P, PACK, S], F32, name="pre")
        fg = w_raw[1]
        rg = [keep.tile([P, 2, H], F32, name="rg%d" % u) for u in range(4)]
        diff = [after_cell3.tile([P, 2, H], F32, name="diff0", offset=0, align_bytes=64)] + [keep.tile([P, 2, H], F32, name="diff%d" % u) for u in range(1, 4)]
        step = [keep.tile([P, 2, H], F32, name="step%d" % u) for u in range(2)]
        step.extend([after_w3.tile([P, 2, H], F32, name="step%d" % u, offset=1024 + 2048 * (u - 2), align_bytes=64) for u in (2, 3)])
        gated = [step[2] if u == 1 else keep.tile([P, 2, H], F32, name="gated%d" % u) for u in range(4)]
        res = keep.tile([P, PACK, S], F32, name="res")
        res_bf = keep.tile([P, S, PACK], BF16, name="res_bf", align_bytes=64)
        res_codes = keep.tile([P, S], U32, name="res_codes", align_bytes=64)
        res_scales = keep.tile([P, S], U8, name="res_scales", align_bytes=64)
        warm = keep.tile([P, 1], F32, name="warm")
        warm2 = keep.tile([P, 1], F32, name="warm2")

        cell_rows = cell.rearrange("(p t) u -> p t u", t=PACK)
        out_rows = out_0.rearrange("(p t) s -> p t s", t=PACK)
        words_out = out_1[0].rearrange("p n t -> p (n t)").bitcast(I32)
        weights = (w1, w2, w3)

        def load_w(i):
            nc.sync.dma_start(out=w_raw[i][:], in_=weights[i].rearrange("(p j) c -> p j c", j=PACK))

        def load_cell(t):
            nc.sync.dma_start(out=cell_sb[t][:], in_=cell_rows[:, t, :])

        nc.vector.memset(xs_all[:].bitcast(I32), 0)
        nc.vector.memset(warm[:], 0.0)
        nc.sync.dma_start(offs_sb[:], offs)
        nc.sync.dma_start(out=xw_all[:].bitcast(I32), in_=x_words[0].rearrange("p n t -> p (n t)").bitcast(I32))
        for q in range(4):
            nc.sync.dma_start(out=xs_all[32 * q : 32 * q + 4, :].bitcast(I32), in_=x_scales[0, 4 * q : 4 * q + 4, :].bitcast(I32))
        nc.scalar.activation(warm2[:], warm[:], SIGMOID)
        nc.sync.dma_start(slot_sb[:], slot)
        load_cell(0)
        load_cell(1)
        load_w(0)
        load_cell(2)
        nc.sync.dma_start(out=peep_sb[:], in_=peep.rearrange("(p t) o -> p (t o)", t=PACK))
        load_w(1)
        load_cell(3)
        load_w(2)

        def cast_w(i, h, copy):
            src = w_raw[i][:].rearrange("p j (m t) -> p m j t", t=PACK)[:, :, :, 2 * h : 2 * h + 2]
            copy(out=w_bf[i][h][:].rearrange("p t m j -> p m j t"), in_=src)

        def quant_w(i, h):
            nc.vector.quantize_mx(out=w_codes[i, h][:].bitcast(FP8X4), scales=w_scales[i][h][:], in_=w_bf[i][h][:].rearrange("p t m j -> p (t m j)"))

        def mm(dst, i, t, js):
            cols = slice((t % 2) * P, (t % 2 + 1) * P)
            nc.tensor.matmul_mx(out=dst, lhsT=w_codes[i, t // 2][:, cols].bitcast(FP8X4), lhsT_scale=w_scales[i][t // 2][:, cols],
                                rhs=xw[:, js].bitcast(FP8X4), rhs_scale=xs[:, js], start=True, stop=True)

        def product(i, u, tag):
            acc = psum.tile([P, 2, H], F32, name=tag, tag=tag, bufs=4)
            for k in range(2):
                mm(acc[:, k, :], i, 2 * (u // 2) + k, slice((u % 2) * H, (u % 2 + 1) * H))
            return acc

        def unit(tile4, u, a=0, b=H):
            return tile4[:, 2 * (u // 2) : 2 * (u // 2) + 2, (u % 2) * H + a : (u % 2) * H + b]

        def gather_cell(t):
            nc.vector.tensor_copy(old[:, t, :], cell_sb[t][:].indirect(slot_sb[:]))

        def forget(t):
            z1 = psum.tile([P, S], F32, name="z", tag="z", bufs=4)
            mm(z1[:], 0, t, slice(0, S))
            nc.vector.scalar_tensor_tensor(out=pre[:, t, :], in0=old[:, t, :], scalar=peep_sb[:, t : t + 1], in1=z1[:], op0=MULT, op1=ADD)

        def forget_gate(t):
            nc.scalar.activation(fg[:, t, :], pre[:, t, :], SIGMOID)

        def reset_gate(u):
            z3 = product(2, u, "z")
            nc.scalar.activation(rg[u][:], z3[:], SIGMOID)

        y = {}

        def difference(u):
            nc.vector.tensor_tensor(diff[u][:], unit(old, u), y[u][:], SUB)

        def stepped(u, eng):
            eng.tensor_tensor(step[u][:], unit(fg, u), diff[u][:], MULT)

        def gate(u, eng):
            eng.tensor_tensor(gated[u][:], step[u][:], rg[u][:], MULT)

        def finish(u, a, b):
            nc.vector.tensor_tensor(unit(res, u, a, b), gated[u][:, :, a:b], y[u][:, :, a:b], ADD)

        def round_res(a, b, copy):
            copy(out=res_bf[:, a:b, :].rearrange("p (c i) t -> p c t i", i=4), in_=res[:, :, a:b].rearrange("p t (c i) -> p c t i", i=4))

        def quant_res(a, b):
            nc.vector.quantize_mx(out=res_codes[:, a:b].bitcast(FP8X4), scales=res_scales[:, a:b], in_=res_bf[:, a:b, :].rearrange("p s t -> p (s t)"))

        nc.vector.tensor_copy(xw[:], xw_all[:].indirect(offs_sb[:]))
        nc.vector.tensor_copy(xs[:], xs_all[:].indirect(offs_sb[:]))
        gather_cell(0)
        gather_cell(1)
        cast_w(0, 0, nc.vector.tensor_copy)
        cast_w(0, 1, nc.scalar.copy)
        quant_w(0, 0)
        quant_w(0, 1)
        gather_cell(2)
        for t in range(3):
            forget(t)
        cast_w(1, 0, nc.scalar.copy)
        cast_w(1, 1, nc.scalar.copy)
        quant_w(1, 0)
        gather_cell(3)
        quant_w(1, 1)
        for u in range(4):
            y[u] = product(1, u, "y")
        for t in range(3):
            forget_gate(t)
        difference(0)
        stepped(0, nc.gpsimd)
        forget(3)
        difference(1)
        stepped(1, nc.gpsimd)
        cast_w(2, 0, nc.scalar.copy)
        forget_gate(3)
        cast_w(2, 1, nc.scalar.copy)
        difference(2)
        difference(3)
        quant_w(2, 0)
        quant_w(2, 1)
        for u in (0, 2, 1, 3):
            reset_gate(u)
        stepped(2, nc.vector)
        stepped(3, nc.vector)
        gate(0, nc.vector)
        gate(2, nc.vector)
        gate(1, nc.gpsimd)
        finish(0, 0, H)
        finish(2, 0, H)
        nc.sync.dma_start(out=out_rows[:, :, 0:H], in_=res[:, :, 0:H])
        round_res(0, H, nc.scalar.copy)
        gate(3, nc.vector)
        finish(1, 0, P)
        finish(3, 0, P)
        nc.sync.dma_start(out=out_rows[:, :, H : H + P], in_=res[:, :, H : H + P])
        round_res(H, H + P, nc.scalar.copy)
        finish(1, P, H)
        finish(3, P, H)
        nc.sync.dma_start(out=out_rows[:, :, H + P : S], in_=res[:, :, H + P : S])
        quant_res(0, H)
        nc.sync.dma_start(out=words_out[:, 0:H], in_=res_codes[:, 0:H].bitcast(I32))
        round_res(H + P, S, nc.vector.tensor_copy)
        quant_res(H, H + P)
        quant_res(H + P, S)
        nc.sync.dma_start(out=words_out[:, H:S], in_=res_codes[:, H:S].bitcast(I32))
        for q in range(4):
            eng = nc.scalar if q % 2 else nc.sync
            eng.dma_start(out=out_2[0, 4 * q : 4 * q + 4, :].bitcast(I32), in_=res_scales[32 * q : 32 * q + 4, :].bitcast(I32))
